import numpy as np
CORES = [2,3,10,11,18,19,26,27,34,35,42,43,50,51,58,59]
N = 16
GROUPS = [[0,1,2,3],[4,5,6,7],[8,9,10,11],[12,13,14,15]]
def setup_inputs(rng):
    return {"x": rng.standard_normal((N, 128, 128), dtype=np.float32)}
def reference(x):
    y = np.empty((N, 128, 128), x.dtype)
    for g in GROUPS:
        s = x[g].max(axis=0)
        for r in g:
            y[r] = s
    return {"y": y}

from concourse.bass import DstId, RemoteDMATransfer

QUARTERS = 4
WIDTH = 32

SCRATCH = {
    "xs": ("dram", [QUARTERS, 128, WIDTH], "float32"),
    "part": ("dram", [3, 128, WIDTH], "float32"),
    "res": ("dram", [QUARTERS, 128, WIDTH], "float32"),
}
SEMAPHORES = [
    "loaded",
    "got_x",
    "got_p",
    "got_res",
    "sent",
    "stored",
]

MAX = 2
ON_CHIP = 0xFFFF
OFF_CHIP = 0x00FF


def rank_program(g, core, T, topo):
    chip = topo.chip(core)
    k = core % topo.CORES_PER_CHIP
    here = chip * topo.CORES_PER_CHIP
    mate = (chip ^ 1) * topo.CORES_PER_CHIP
    ranks = [c for c in T.cores if topo.chip(c) == chip]
    sem = T.sem

    def to(c):
        rid, pid, _se = topo.addr(c)
        return DstId(rid=rid, pnc=pid)

    if core in ranks:
        i = ranks.index(core)
        peer = ranks[1 - i]
        g.sync.dma_start(T.xs[:], T.x[:]).then_inc(sem.loaded, 16)
        g.wait_ge(sem.loaded, 16)
        g.remote_dma_fused([
            RemoteDMATransfer(dst_ids=[to(peer)], dma_engine_mask=0x000F, remote_sem=sem.got_x,
                              src=T.xs[1 - i], dst=T.part[0]),
            RemoteDMATransfer(dst_ids=[to(here + 6)], dma_engine_mask=0x00F0, remote_sem=sem.got_x,
                              src=T.xs[2], dst=T.part[i]),
            RemoteDMATransfer(dst_ids=[to(here + 7)], dma_engine_mask=0x0F00, remote_sem=sem.got_x,
                              src=T.xs[3], dst=T.part[i]),
        ], local_sem=sem.sent)
        g.wait_ge(sem.got_x, 4)
        g.remote_dma_fused([
            RemoteDMATransfer(dst_ids=[to(here + i), to(mate + i)], dma_engine_mask=OFF_CHIP, remote_sem=sem.got_p,
                              srcs=[T.xs[i], T.part[0]], dsts=[T.part[0], T.part[1]], alu_op=MAX),
        ], local_sem=sem.sent)
        g.sync.wait_ge(sem.got_res, 4 * 16)
        g.sync.dma_start(T.y[:], T.res[:]).then_inc(sem.stored, 16)
        g.sync.wait_ge(sem.stored, 16)
        g.wait_ge(sem.sent, 12 + 8)
        return

    if k in (0, 1):
        g.wait_ge(sem.got_p, 8 + 8)
        g.remote_dma_fused([
            RemoteDMATransfer(dst_ids=[to(c) for c in ranks], dma_engine_mask=ON_CHIP, remote_sem=sem.got_res,
                              srcs=[T.part[0], T.part[1]], dsts=[T.res[k], T.res[k]], alu_op=MAX),
        ], local_sem=sem.sent)
        g.wait_ge(sem.sent, 16)
        return

    if k in (6, 7):
        q = k - 4
        g.wait_ge(sem.got_x, 4 + 4)
        g.remote_dma_fused([
            RemoteDMATransfer(dst_ids=[to(mate + k)], dma_engine_mask=OFF_CHIP, remote_sem=sem.got_p,
                              srcs=[T.part[0], T.part[1]], dsts=[T.part[2]], alu_op=MAX),
        ], local_sem=sem.sent)
        g.wait_ge(sem.got_p, 8)
        g.remote_dma_fused([
            RemoteDMATransfer(dst_ids=[to(c) for c in ranks], dma_engine_mask=ON_CHIP, remote_sem=sem.got_res,
                              srcs=[T.part[0], T.part[1], T.part[2]], dsts=[T.res[q], T.res[q]], alu_op=MAX),
        ], local_sem=sem.sent)
        g.wait_ge(sem.sent, 8 + 16)
        return
